import numpy as np
import ml_dtypes


def mxq(x, axis, fmt="e4m3"):
    dtype, down = {"e4m3": (ml_dtypes.float8_e4m3fn, 7), "e5m2": (ml_dtypes.float8_e5m2, 14)}[fmt]
    v = np.moveaxis(np.asarray(x, np.float32).astype(ml_dtypes.bfloat16).astype(np.float64), axis, -1)
    blocks = v.reshape(v.shape[:-1] + (-1, 32))
    amax = np.abs(blocks).max(-1, keepdims=True)
    byte = np.maximum(np.where(amax > 0, np.frexp(amax)[1] - 1 + 127, 0) - down, 1)
    scale = np.exp2(byte - 127.0)
    codes = (blocks / scale).astype(np.float32).astype(dtype).astype(np.float64)
    return np.moveaxis((codes * scale).reshape(v.shape), -1, axis)


WIDE = False


def mx_kscale(k):
    if not WIDE:
        return np.ones(k)
    levels = np.array([10, -10, 5, -5, 0])
    if k % 512:
        return np.exp2(np.random.permutation(np.resize(levels, k // 32))).repeat(32)
    a = np.empty((k // 512, 16))
    for p in range(k // 512):
        a[p, :8] = np.random.permutation(np.resize(levels, 8))
        for g in range(8):
            far = levels[np.abs(levels - a[p, g]) >= 10]
            a[p, g + 8] = far[np.random.randint(len(far))]
    return np.exp2(a.ravel()).repeat(32)


def f64(x):
    return np.asarray(x).astype(np.float64)


def striped(idx):
    return np.tile(idx.reshape(-1, 16).T, (8, 1)).astype(np.uint16)


def unstriped(offs):
    return offs[:16].T.reshape(-1).astype(np.int64)


E2M1 = np.array([0.0, 0.5, 1.0, 1.5, 2.0, 3.0, 4.0, 6.0, -0.0, -0.5, -1.0, -1.5, -2.0, -3.0, -4.0, -6.0])


def pack_weight(w, fmt):
    k, n = w.shape
    w = f64(np.asarray(w, np.float32).astype(ml_dtypes.bfloat16)).reshape(k // 32, 32, n)
    amax = np.abs(w).max(1)
    if fmt == "e4m3":
        byte = np.frexp(amax)[1] - 1 + 127 - 7
    else:
        mant, ex = np.frexp(amax / 6.0)
        byte = np.where(mant > 0.5, ex, ex - 1) + 127
    byte = np.clip(np.where(amax > 0, byte, 1), 1, 254)
    scaled = (w * np.exp2(127.0 - byte)[:, None, :]).reshape(k, n).astype(np.float32)
    by_word = np.ascontiguousarray(scaled.reshape(k // 512, 128, 4, n).transpose(0, 1, 3, 2))
    if fmt == "e4m3":
        words = by_word.astype(ml_dtypes.float8_e4m3fn).view(np.uint8)
    else:
        c = by_word.astype(ml_dtypes.float4_e2m1fn).view(np.uint8) & 0xF
        words = (c[..., 0::2] | (c[..., 1::2] << 4)).reshape(k // 512, 128, 2 * n)
    return np.ascontiguousarray(words), np.ascontiguousarray(byte.astype(np.uint8).reshape(k // 512, 16, n))


def unpack_weight(words, scales, fmt):
    g, _, n = scales.shape
    words = np.ascontiguousarray(words).reshape(g, 128, n, -1)
    if fmt == "e4m3":
        vals = words.view(ml_dtypes.float8_e4m3fn).astype(np.float64)
    else:
        nib = np.empty((g, 128, n, 4), np.uint8)
        nib[..., 0::2] = words & 0xF
        nib[..., 1::2] = words >> 4
        vals = E2M1[nib]
    vals = vals * np.repeat(np.exp2(scales.astype(np.float64) - 127.0), 8, axis=1)[..., None]
    return vals.transpose(0, 1, 3, 2).reshape(g * 512, n)


def gelu(v):
    return 0.5 * v * (1.0 + np.tanh(np.sqrt(2.0 / np.pi) * (v + 0.044715 * v**3)))


K, H, T, S, P = 1024, 1024, 4096, 1024, 512

def setup_inputs():
    n = np.random.standard_normal
    s = mx_kscale(K)[:, None]
    u = mx_kscale(H)[:, None]
    tab_words, tab_scales = pack_weight(n((K, T)) * s, "e4m3")
    w4_words, w4_scales = pack_weight(1.3 * n((K, H)) / np.sqrt(K) / s, "e2m1")
    return {
        "tab_words": tab_words, "tab_scales": tab_scales,
        "offs": striped(np.random.permutation(T)[:S]),
        "pos1": striped(np.random.permutation(S)[:P]),
        "pos2": striped(np.random.permutation(S)[:P]),
        "w1": (n((K, H)) / np.sqrt(K) / s * u.T).astype(np.float32),
        "w4_words": w4_words, "w4_scales": w4_scales,
        "low": (0.6 * n(H) * u[:, 0]).astype(np.float32),
        "gain": (6.0 * np.exp(0.3 * n(H)) / np.sqrt(H) / u[:, 0] ** 2).astype(np.float32),
    }

def reference(tab_words, tab_scales, offs, pos1, pos2, w1, w4_words, w4_scales, low, gain):
    v = unpack_weight(tab_words, tab_scales, "e4m3")[:, unstriped(offs)]
    w4 = unpack_weight(w4_words, w4_scales, "e2m1")
    a = mxq(f64(w1), 0, "e4m3").T @ v
    b = w4.T @ v
    h = np.maximum(a, f64(low)[:, None]) * np.tanh(b)
    x1 = mxq(h[:, unstriped(pos1)], 0, "e4m3")
    xs = h[:, unstriped(pos2)] * f64(gain)[:, None]
    x2 = np.abs(xs)
    e = x1.T @ mxq(x2, 0, "e4m3")
    d = x1.T @ mxq(xs, 0, "e4m3")
    return e / (1.0 + np.exp(-d))

@@ -1,0 +1,309 @@
+from contextlib import ExitStack
+
+import concourse.mybir as mybir
+from concourse.masks import make_identity
+
+K, H, T, S, M = 1024, 1024, 4096, 1024, 512
+FLOPS = 2 * (2 * K * H * S + 2 * H * M * M)
+
+F32 = mybir.dt.float32
+BF16 = mybir.dt.bfloat16
+I32 = mybir.dt.int32
+U32 = mybir.dt.uint32
+U16 = mybir.dt.uint16
+U8 = mybir.dt.uint8
+FP8X4 = mybir.dt.float8_e4m3fn_x4
+FP4X4 = mybir.dt.float4_e2m1fn_x4
+ACT = mybir.ActivationFunctionType
+ALU = mybir.AluOpType
+
+P = 128
+PACK = 4
+PASS = P * PACK
+BANK = 512
+K_PASSES = K // PASS
+R_PASSES = H // PASS
+HALVES = S // BANK
+ROW_TILES = R_PASSES * PACK
+M_TILES = M // P
+
+
+def tile_list_isogloss_shared_features_kernel(
+    tc, tab_words, tab_scales, offs, pos1, pos2, w1, w4_words, w4_scales, low, gain, out
+):
+    nc = tc.nc
+    with ExitStack() as ctx:
+        keep = ctx.enter_context(tc.tile_pool(name="keep", bufs=1))
+        shared = ctx.enter_context(tc.tile_pool(name="shared", bufs=1))
+        psum = ctx.enter_context(tc.psum_pool(name="psum", bufs=4))
+
+        offs_sb = keep.tile([P, S // 16], U16, name="offs_sb")
+        pos1_sb = keep.tile([P, M // 16], U16, name="pos1_sb")
+        pos2_sb = keep.tile([P, M // 16], U16, name="pos2_sb")
+
+        tab_sc = keep.tile([P, K_PASSES, T], U8, name="tab_sc", align_bytes=64)
+        nc.vector.memset(tab_sc[:, 0, :].bitcast(I32), 0)
+        nc.gpsimd.memset(tab_sc[:, 1, :].bitcast(I32), 0)
+        w4_sc = keep.tile([P, K_PASSES, H], U8, name="w4_sc", align_bytes=64)
+        nc.vector.memset(w4_sc[:].bitcast(I32), 0)
+        rows = keep.tile([P, R_PASSES * P], F32, name="rows")
+        nc.vector.memset(rows[:], 0.0)
+        ident = keep.tile([P, P], F32, name="ident")
+        make_identity(nc, ident[:])
+
+        tab = [keep.tile([P, T], I32, name="tab%d" % a, tag="tab%d" % a, align_bytes=64) for a in range(K_PASSES)]
+        w4_raw = keep.tile([P, K_PASSES, 2 * H // 4], I32, name="w4_raw")
+        w1_raw = {}
+        for b in range(R_PASSES):
+            for a in range(K_PASSES):
+                w1_raw[b, a] = keep.tile([P, PACK, PASS], F32, name="w1_raw%d%d" % (b, a))
+
+        def load_tab(a):
+            nc.sync.dma_start(out=tab[a][:], in_=tab_words[a].rearrange("p t i -> p (t i)").bitcast(I32))
+
+        def load_w1(b, a):
+            nc.sync.dma_start(
+                out=w1_raw[b, a][:],
+                in_=w1[a * PASS : (a + 1) * PASS, b * PASS : (b + 1) * PASS].rearrange("(p j) c -> p j c", j=PACK),
+            )
+
+        def load_scale_rows(dst, src):
+            for q in range(4):
+                nc.sync.dma_start(
+                    out=dst[32 * q : 32 * q + 4, :, :].bitcast(I32),
+                    in_=src[:, 4 * q : 4 * q + 4, :].bitcast(I32).rearrange("a r c -> r a c"),
+                )
+
+        nc.sync.dma_start(offs_sb[:], offs)
+        nc.sync.dma_start(out=w4_raw[:], in_=w4_words.bitcast(I32).rearrange("a p c -> p a c"))
+        load_scale_rows(tab_sc, tab_scales)
+        load_tab(0)
+        load_scale_rows(w4_sc, w4_scales)
+        load_tab(1)
+        for n, vec in enumerate((low, gain)):
+            nc.sync.dma_start(
+                out=rows[PACK * n : PACK * (n + 1), :].rearrange("t (n i) -> t n i", i=8),
+                in_=vec.rearrange("(n t i) -> t n i", t=PACK, i=8),
+            )
+        load_w1(0, 0)
+        load_w1(0, 1)
+        nc.sync.dma_start(pos2_sb[:], pos2)
+        nc.sync.dma_start(pos1_sb[:], pos1)
+        load_w1(1, 0)
+        load_w1(1, 1)
+
+        v_words, v_scales = {}, {}
+
+        def gather_words(a):
+            for s in range(HALVES):
+                v_words[a, s] = keep.tile([P, BANK], U32, name="v_words%d%d" % (a, s), align_bytes=64)
+                nc.vector.tensor_copy(
+                    v_words[a, s][:], tab[a][:].bitcast(U32).indirect(offs_sb[:, 32 * s : 32 * (s + 1)])
+                )
+
+        def gather_scales(a):
+            v_scales[a] = keep.tile([P, S], U8, name="v_scales%d" % a, align_bytes=64)
+            nc.vector.tensor_copy(v_scales[a][:], tab_sc[:, a, :].indirect(offs_sb[:]))
+
+        gather_scales(0)
+        gather_scales(1)
+        gather_words(0)
+
+        w4_codes = keep.tile([P, K_PASSES * ROW_TILES, 2 * P], U8, name="w4_codes", align_bytes=64)
+        w4_plane = keep.tile([P, K_PASSES * ROW_TILES, P], U8, name="w4_plane", align_bytes=64)
+        nc.vector.tensor_copy(
+            w4_codes[:].bitcast(I32).rearrange("p (g t) (q w) -> p g t q w", t=PACK, w=4),
+            w4_raw[:].rearrange("p a (b q t w) -> p (a b) t q w", b=R_PASSES, t=PACK, w=4),
+        )
+        nc.vector.tensor_copy(
+            w4_plane[:].bitcast(I32).rearrange("p (g t) (q w) -> p g t q w", t=PACK, w=2),
+            w4_sc[:].bitcast(I32).rearrange("p a (b q t w) -> p (a b) t q w", b=R_PASSES, t=PACK, w=2),
+        )
+        gather_words(1)
+
+        turned = psum.tile([P, R_PASSES, P], F32, name="turned", tag="a")
+        for b in range(R_PASSES):
+            nc.tensor.transpose(turned[:, b, :], rows[:, b * P : (b + 1) * P], ident[:])
+        consts = keep.tile([P, R_PASSES, 2 * PACK], F32, name="consts")
+        nc.scalar.copy(consts[:], turned[:, :, 0 : 2 * PACK])
+
+        w1_grouped, w1_codes, w1_plane = {}, {}, {}
+
+        def round_w1(b, a, t, copy, dst):
+            copy(
+                dst.rearrange("p (q u i j) -> p q u j i", u=2, i=4, j=PACK),
+                w1_raw[b, a][:].rearrange("p j (q t u i) -> p t q u j i", t=PACK, u=2, i=4)[:, t],
+            )
+
+        def quantise(src, words, name):
+            codes = keep.tile([P, words], U32, name=name + "_codes", align_bytes=64)
+            plane = keep.tile([P, words], U8, name=name + "_plane", align_bytes=64)
+            nc.vector.quantize_mx(out=codes[:].bitcast(FP8X4), scales=plane[:], in_=src)
+            return codes, plane
+
+        def quantise_w1(b, a, t):
+            codes, plane = quantise(w1_grouped[b, a, t][:], P, "w1_%d%d%d" % (b, a, t))
+            w1_codes[b, a, t], w1_plane[b, a, t] = codes[:], plane[:]
+
+        def late_w1(t):
+            both = keep.tile([P, K_PASSES * PASS], BF16, name="w1_both", tag="w1_both", bufs=2, align_bytes=64)
+            for a in range(K_PASSES):
+                round_w1(1, a, t, nc.scalar.copy, both[:, a * PASS : (a + 1) * PASS])
+            codes, plane = quantise(both[:], K_PASSES * P, "w1_late%d" % t)
+            for a in range(K_PASSES):
+                w1_codes[1, a, t], w1_plane[1, a, t] = codes[:, a * P : (a + 1) * P], plane[:, a * P : (a + 1) * P]
+
+        steps = [(a, t) for a in range(K_PASSES) for t in range(PACK)]
+        for n, (a, t) in enumerate(steps):
+            w1_grouped[0, a, t] = keep.tile([P, PASS], BF16, name="w1_grouped", tag="w1_grouped", bufs=4, align_bytes=64)
+            round_w1(0, a, t, nc.vector.tensor_copy, w1_grouped[0, a, t][:])
+            if n > 0:
+                quantise_w1(0, *steps[n - 1])
+        quantise_w1(0, *steps[-1])
+
+        late_tanh = shared.tile([P, PACK * S], F32, name="late_tanh", offset=0)
+        tanh_b, h = {}, {}
+
+        def tanh_tile(n):
+            if n < PACK:
+                tanh_b[n] = keep.tile([P, S], F32, name="tanh%d" % n, tag="tanh%d" % n, align_bytes=64)[:]
+            else:
+                tanh_b[n] = late_tanh[:, (n - PACK) * S : (n - PACK + 1) * S]
+            for s in range(HALVES):
+                acc = psum.tile([P, BANK], F32, name="acc_b", tag="b")
+                for a in range(K_PASSES):
+                    nc.tensor.matmul_mx(
+                        out=acc[:],
+                        lhsT=w4_codes[:, a * ROW_TILES + n, :].bitcast(FP4X4),
+                        lhsT_scale=w4_plane[:, a * ROW_TILES + n, :],
+                        rhs=v_words[a, s][:].bitcast(FP8X4),
+                        rhs_scale=v_scales[a][:, s * BANK : (s + 1) * BANK],
+                        start=(a == 0),
+                        stop=(a == K_PASSES - 1),
+                    )
+                nc.scalar.activation(tanh_b[n][:, s * BANK : (s + 1) * BANK], acc[:], ACT.Tanh)
+
+        def h_tile(n):
+            b, t = divmod(n, PACK)
+            h[n] = keep.tile([P, S], F32, name="h%d" % n)
+            for s in range(HALVES):
+                acc = psum.tile([P, BANK], F32, name="acc_a", tag="a")
+                for a in range(K_PASSES):
+                    nc.tensor.matmul_mx(
+                        out=acc[:],
+                        lhsT=w1_codes[b, a, t].bitcast(FP8X4),
+                        lhsT_scale=w1_plane[b, a, t],
+                        rhs=v_words[a, s][:].bitcast(FP8X4),
+                        rhs_scale=v_scales[a][:, s * BANK : (s + 1) * BANK],
+                        start=(a == 0),
+                        stop=(a == K_PASSES - 1),
+                    )
+                cols = slice(s * BANK, (s + 1) * BANK)
+                nc.vector.scalar_tensor_tensor(
+                    h[n][:, cols], acc[:], consts[:, b, t : t + 1], tanh_b[n][:, cols], ALU.max, ALU.mult
+                )
+
+        south, south_planes, xs, x2 = {}, {}, {}, {}
+
+        def pick_south(n):
+            b, t = divmod(n, PACK)
+            if t == 0:
+                south[b] = keep.tile([P, PACK * M], F32, name="south%d" % b, tag="tab%d" % b, align_bytes=64)
+                south_planes[b] = keep.tile(
+                    [P, PACK * M], BF16, name="south_planes%d" % b, tag="tanh%d" % (3 * b), align_bytes=64
+                )
+            cols = slice(t * M, (t + 1) * M)
+            nc.vector.tensor_copy(south[b][:, cols], h[n][:].indirect(pos2_sb[:]))
+            nc.scalar.activation(
+                south_planes[b][:, cols], south[b][:, cols], ACT.Copy, scale=consts[:, b, PACK + t : PACK + t + 1]
+            )
+
+        def weave(dst, src):
+            nc.scalar.copy(
+                dst.rearrange("p (c i t) -> p c t i", i=4, t=PACK),
+                src.rearrange("p (t c i) -> p c t i", i=4, t=PACK),
+            )
+
+        def quantise_south(b):
+            tags = ("tanh1", "tanh2") if b == 0 else ("signed", "magnitude")
+            signed = keep.tile([P, PACK * M], BF16, name="signed%d" % b, tag=tags[0], align_bytes=64)
+            magnitude = keep.tile([P, PACK * M], BF16, name="magnitude%d" % b, tag=tags[1], align_bytes=64)
+            weave(signed[:], south_planes[b][:])
+            nc.scalar.activation(magnitude[:], signed[:], ACT.Abs)
+            xs[b] = quantise(signed[:], M, "xs%d" % b)
+            x2[b] = quantise(magnitude[:], M, "x2%d" % b)
+
+        tanh_tile(0)
+        tanh_tile(1)
+        for n in range(ROW_TILES):
+            h_tile(n)
+            if n + 2 < ROW_TILES:
+                tanh_tile(n + 2)
+            if n < PACK:
+                late_w1(n)
+            if n > 0:
+                pick_south(n - 1)
+            if n == PACK:
+                quantise_south(0)
+        pick_south(ROW_TILES - 1)
+        quantise_south(1)
+
+        groups = ((0, 3), (3, 4))
+        woven, x1 = {}, {}
+
+        def pick_north(g, b):
+            m0, m1 = groups[g]
+            width = (m1 - m0) * P
+            north = shared.tile([P, PACK * width], F32, name="north%d%d" % (g, b), offset=b * 2 * S * 4)
+            for t in range(PACK):
+                nc.vector.tensor_copy(
+                    north[:, t * width : (t + 1) * width], h[b * PACK + t][:].indirect(pos1_sb[:, 8 * m0 : 8 * m1])
+                )
+            woven[g, b] = keep.tile([P, PACK * width], BF16, name="north_woven%d%d" % (g, b), align_bytes=64)
+            weave(woven[g, b][:], north[:])
+
+        def quantise_north(g, b):
+            m0, m1 = groups[g]
+            codes, plane = quantise(woven[g, b][:], (m1 - m0) * P, "x1_%d%d" % (g, b))
+            for m in range(m0, m1):
+                cols = slice((m - m0) * P, (m - m0 + 1) * P)
+                x1[m, b] = codes[:, cols], plane[:, cols]
+
+        sums = {}
+
+        def multiply(g, b):
+            for m in range(*groups[g]):
+                for tag, south_q in (("b", xs), ("a", x2)):
+                    if b == 0:
+                        sums[m, tag] = psum.tile([P, M], F32, name="acc_" + tag, tag=tag)
+                    nc.tensor.matmul_mx(
+                        out=sums[m, tag][:],
+                        lhsT=x1[m, b][0].bitcast(FP8X4),
+                        lhsT_scale=x1[m, b][1],
+                        rhs=south_q[b][0][:].bitcast(FP8X4),
+                        rhs_scale=south_q[b][1][:],
+                        start=(b == 0),
+                        stop=(b == R_PASSES - 1),
+                    )
+
+        def score(m):
+            weight = keep.tile([P, M], F32, name="weight", tag="weight", bufs=2)
+            nc.scalar.activation(weight[:], sums[m, "b"][:], ACT.Sigmoid)
+            result = keep.tile([P, M], F32, name="result%d" % m)
+            nc.vector.tensor_tensor(result[:], sums[m, "a"][:], weight[:], ALU.mult)
+            nc.sync.dma_start(out=out[m * P : (m + 1) * P, :], in_=result[:])
+
+        pick_north(0, 0)
+        pick_north(0, 1)
+        quantise_north(0, 0)
+        multiply(0, 0)
+        pick_north(1, 0)
+        quantise_north(0, 1)
+        multiply(0, 1)
+        pick_north(1, 1)
+        quantise_north(1, 0)
+        multiply(1, 0)
+        quantise_north(1, 1)
+        multiply(1, 1)
+        for m in range(M_TILES):
+            score(m)

@@ -20,12 +20,24 @@ ALU = mybir.AluOpType
 P = 128
 PACK = 4
 PASS = P * PACK
+RUN = 8
 BANK = 512
+LIST_ROWS = 16
+QUADRANT = 32
+SCALE_ROWS = PASS // 32
 K_PASSES = K // PASS
 R_PASSES = H // PASS
 HALVES = S // BANK
 ROW_TILES = R_PASSES * PACK
 M_TILES = M // P
+ALIGN = 64
+
+LATE_TANH_AT = 0
+SIGNED_AT = PACK * S * 4
+MAGNITUDE_AT = SIGNED_AT + PACK * M * 2
+NORTH_AT = (LATE_TANH_AT, SIGNED_AT - 1024)
+
+NORTH_GROUPS = ((0, M_TILES - 1), (M_TILES - 1, M_TILES))
 
 
 def tile_list_isogloss_shared_features_kernel(
@@ -35,188 +47,216 @@ def tile_list_isogloss_shared_features_kernel(
     with ExitStack() as ctx:
         keep = ctx.enter_context(tc.tile_pool(name="keep", bufs=1))
         shared = ctx.enter_context(tc.tile_pool(name="shared", bufs=1))
-        psum = ctx.enter_context(tc.psum_pool(name="psum", bufs=4))
+        psum = ctx.enter_context(tc.psum_pool(name="psum", bufs=1))
 
-        offs_sb = keep.tile([P, S // 16], U16, name="offs_sb")
-        pos1_sb = keep.tile([P, M // 16], U16, name="pos1_sb")
-        pos2_sb = keep.tile([P, M // 16], U16, name="pos2_sb")
+        def bank_tag(pair, which):
+            return "bank%d" % (2 * pair + which)
 
-        tab_sc = keep.tile([P, K_PASSES, T], U8, name="tab_sc", align_bytes=64)
-        nc.vector.memset(tab_sc[:, 0, :].bitcast(I32), 0)
-        nc.gpsimd.memset(tab_sc[:, 1, :].bitcast(I32), 0)
-        w4_sc = keep.tile([P, K_PASSES, H], U8, name="w4_sc", align_bytes=64)
-        nc.vector.memset(w4_sc[:].bitcast(I32), 0)
-        rows = keep.tile([P, R_PASSES * P], F32, name="rows")
-        nc.vector.memset(rows[:], 0.0)
+        offs_sb = keep.tile([P, S // LIST_ROWS], U16, name="offs_sb")
+        pos1_sb = keep.tile([P, M // LIST_ROWS], U16, name="pos1_sb")
+        pos2_sb = keep.tile([P, M // LIST_ROWS], U16, name="pos2_sb")
+
+        all_rows = K_PASSES * SCALE_ROWS
+        tab_rows = keep.tile([P, T], U8, name="tab_rows", align_bytes=ALIGN)
+        nc.vector.memset(tab_rows[all_rows : P // 2, :].bitcast(I32), 0)
+        nc.vector.memset(tab_rows[P // 2 : P, :].bitcast(I32), 0)
+        w4_rows = keep.tile([all_rows, H // 4], I32, name="w4_rows")
+        planes = keep.tile([P, K_PASSES, S + H], U8, name="planes", align_bytes=ALIGN)
+        nc.gpsimd.memset(planes[:].bitcast(I32), 0)
+        vectors = keep.tile([2, H], F32, name="vectors")
+        vectors_dealt = keep.tile([P, H], F32, name="vectors_dealt")
+        nc.gpsimd.memset(vectors_dealt[:], 0.0)
         ident = keep.tile([P, P], F32, name="ident")
         make_identity(nc, ident[:])
 
-        tab = [keep.tile([P, T], I32, name="tab%d" % a, tag="tab%d" % a, align_bytes=64) for a in range(K_PASSES)]
-        w4_raw = keep.tile([P, K_PASSES, 2 * H // 4], I32, name="w4_raw")
+        warm_in = keep.tile([P, 1], F32, name="warm_in")
+        warm_out = keep.tile([P, 1], F32, name="warm_out")
+        nc.vector.memset(warm_in[:], 0.0)
+        nc.scalar.activation(warm_out[:], warm_in[:], ACT.Sigmoid)
+
+        tab = [keep.tile([P, T], I32, name="tab%d" % a, tag="tab%d" % a, align_bytes=ALIGN) for a in range(K_PASSES)]
+        w4_raw = [keep.tile([P, K_PASSES, 2 * PASS // 4], I32, name="w4_raw%d" % b) for b in range(R_PASSES)]
         w1_raw = {}
-        for b in range(R_PASSES):
-            for a in range(K_PASSES):
-                w1_raw[b, a] = keep.tile([P, PACK, PASS], F32, name="w1_raw%d%d" % (b, a))
 
         def load_tab(a):
             nc.sync.dma_start(out=tab[a][:], in_=tab_words[a].rearrange("p t i -> p (t i)").bitcast(I32))
 
-        def load_w1(b, a):
+        def load_w1(b, a, tag):
+            w1_raw[b, a] = keep.tile([P, PACK, PASS], F32, name="w1_raw%d%d" % (b, a), tag=tag)
             nc.sync.dma_start(
                 out=w1_raw[b, a][:],
                 in_=w1[a * PASS : (a + 1) * PASS, b * PASS : (b + 1) * PASS].rearrange("(p j) c -> p j c", j=PACK),
             )
 
-        def load_scale_rows(dst, src):
-            for q in range(4):
-                nc.sync.dma_start(
-                    out=dst[32 * q : 32 * q + 4, :, :].bitcast(I32),
-                    in_=src[:, 4 * q : 4 * q + 4, :].bitcast(I32).rearrange("a r c -> r a c"),
-                )
+        def load_w4(b):
+            nc.sync.dma_start(
+                out=w4_raw[b][:],
+                in_=w4_words[:, :, b * 2 * PASS : (b + 1) * 2 * PASS].bitcast(I32).rearrange("a p c -> p a c"),
+            )
 
         nc.sync.dma_start(offs_sb[:], offs)
-        nc.sync.dma_start(out=w4_raw[:], in_=w4_words.bitcast(I32).rearrange("a p c -> p a c"))
-        load_scale_rows(tab_sc, tab_scales)
+        nc.sync.dma_start(
+            out=tab_rows[0:all_rows, :].bitcast(I32), in_=tab_scales.bitcast(I32).rearrange("a q c -> (a q) c")
+        )
+        nc.sync.dma_start(out=w4_rows[:], in_=w4_scales.bitcast(I32).rearrange("a q c -> (a q) c"))
+        for row, vec in enumerate((low, gain)):
+            nc.sync.dma_start(out=vectors[row : row + 1, :], in_=vec.rearrange("(o r) -> o r", o=1))
+        load_w4(0)
         load_tab(0)
-        load_scale_rows(w4_sc, w4_scales)
-        load_tab(1)
-        for n, vec in enumerate((low, gain)):
-            nc.sync.dma_start(
-                out=rows[PACK * n : PACK * (n + 1), :].rearrange("t (n i) -> t n i", i=8),
-                in_=vec.rearrange("(n t i) -> t n i", t=PACK, i=8),
-            )
-        load_w1(0, 0)
-        load_w1(0, 1)
         nc.sync.dma_start(pos2_sb[:], pos2)
         nc.sync.dma_start(pos1_sb[:], pos1)
-        load_w1(1, 0)
-        load_w1(1, 1)
+        load_tab(1)
+        load_w1(0, 0, "w1_first")
+        load_w1(0, 1, "w1_second")
+        load_w4(1)
 
-        v_words, v_scales = {}, {}
+        picked_rows = keep.tile([P, S], U8, name="picked_rows", align_bytes=ALIGN)
+        nc.vector.tensor_copy(picked_rows[:], tab_rows[:].indirect(offs_sb[:]))
+        staged = keep.tile([all_rows, (S + H) // 4], I32, name="staged", tag="staged")
+        nc.vector.tensor_copy(
+            staged[:, S // 4 :].rearrange("p (b t q w) -> p b t q w", b=R_PASSES, t=PACK, w=RUN // 4),
+            w4_rows[:].rearrange("p (b q t w) -> p b t q w", b=R_PASSES, t=PACK, w=RUN // 4),
+        )
+        nc.vector.tensor_copy(staged[:, 0 : S // 4], picked_rows[0:all_rows, :].bitcast(I32))
+        rows_per_quadrant = SCALE_ROWS // (P // QUADRANT)
+        for a, queue in enumerate((nc.scalar, nc.gpsimd)):
+            for r in range(rows_per_quadrant):
+                queue.dma_start(
+                    out=planes[r:P:QUADRANT, a, :].bitcast(I32),
+                    in_=staged[SCALE_ROWS * a + r : SCALE_ROWS * (a + 1) : rows_per_quadrant, :],
+                )
+
+        v_words, w4_codes = {}, {}
 
         def gather_words(a):
             for s in range(HALVES):
-                v_words[a, s] = keep.tile([P, BANK], U32, name="v_words%d%d" % (a, s), align_bytes=64)
-                nc.vector.tensor_copy(
-                    v_words[a, s][:], tab[a][:].bitcast(U32).indirect(offs_sb[:, 32 * s : 32 * (s + 1)])
-                )
+                v_words[a, s] = keep.tile([P, BANK], U32, name="v_words%d%d" % (a, s), align_bytes=ALIGN)
+                entries = offs_sb[:, s * BANK // LIST_ROWS : (s + 1) * BANK // LIST_ROWS]
+                nc.vector.tensor_copy(v_words[a, s][:], tab[a][:].bitcast(U32).indirect(entries))
 
-        def gather_scales(a):
-            v_scales[a] = keep.tile([P, S], U8, name="v_scales%d" % a, align_bytes=64)
-            nc.vector.tensor_copy(v_scales[a][:], tab_sc[:, a, :].indirect(offs_sb[:]))
+        def deal_w4(b, t0, t1, tag):
+            dealt = keep.tile([P, K_PASSES * (t1 - t0), 2 * P], U8, name="w4_dealt", tag=tag, align_bytes=ALIGN)
+            nc.vector.tensor_copy(
+                dealt[:].bitcast(I32).rearrange("p (a t) (q w) -> p a t q w", a=K_PASSES, w=RUN // 2),
+                w4_raw[b][:].rearrange("p a (q t w) -> p a t q w", t=PACK, w=RUN // 2)[:, :, t0:t1],
+            )
+            for a in range(K_PASSES):
+                for t in range(t0, t1):
+                    w4_codes[a, b * PACK + t] = dealt[:, a * (t1 - t0) + t - t0, :]
 
-        gather_scales(0)
-        gather_scales(1)
+        lead = 2
+        deal_w4(0, 0, lead, "w4_first")
         gather_words(0)
-
-        w4_codes = keep.tile([P, K_PASSES * ROW_TILES, 2 * P], U8, name="w4_codes", align_bytes=64)
-        w4_plane = keep.tile([P, K_PASSES * ROW_TILES, P], U8, name="w4_plane", align_bytes=64)
-        nc.vector.tensor_copy(
-            w4_codes[:].bitcast(I32).rearrange("p (g t) (q w) -> p g t q w", t=PACK, w=4),
-            w4_raw[:].rearrange("p a (b q t w) -> p (a b) t q w", b=R_PASSES, t=PACK, w=4),
-        )
-        nc.vector.tensor_copy(
-            w4_plane[:].bitcast(I32).rearrange("p (g t) (q w) -> p g t q w", t=PACK, w=2),
-            w4_sc[:].bitcast(I32).rearrange("p a (b q t w) -> p (a b) t q w", b=R_PASSES, t=PACK, w=2),
-        )
         gather_words(1)
 
-        turned = psum.tile([P, R_PASSES, P], F32, name="turned", tag="a")
+        nc.scalar.copy(
+            vectors_dealt[0:2, :].rearrange("p (b t q i) -> p b t q i", b=R_PASSES, t=PACK, i=RUN),
+            vectors[:].rearrange("p (b q t i) -> p b t q i", b=R_PASSES, t=PACK, i=RUN),
+        )
+        consts = keep.tile([P, ROW_TILES, 2], F32, name="consts")
         for b in range(R_PASSES):
-            nc.tensor.transpose(turned[:, b, :], rows[:, b * P : (b + 1) * P], ident[:])
-        consts = keep.tile([P, R_PASSES, 2 * PACK], F32, name="consts")
-        nc.scalar.copy(consts[:], turned[:, :, 0 : 2 * PACK])
+            turned = psum.tile([P, PACK, P], F32, name="turned", tag=bank_tag(3, b))
+            for t in range(PACK):
+                n = b * PACK + t
+                nc.tensor.transpose(turned[:, t, :], vectors_dealt[:, n * P : (n + 1) * P], ident[:])
+            nc.scalar.copy(consts[:, b * PACK : (b + 1) * PACK, :], turned[:, :, 0:2])
 
-        w1_grouped, w1_codes, w1_plane = {}, {}, {}
+        w1_rounded, w1_codes, w1_plane = {}, {}, {}
 
-        def round_w1(b, a, t, copy, dst):
-            copy(
-                dst.rearrange("p (q u i j) -> p q u j i", u=2, i=4, j=PACK),
-                w1_raw[b, a][:].rearrange("p j (q t u i) -> p t q u j i", t=PACK, u=2, i=4)[:, t],
-            )
-
-        def quantise(src, words, name):
-            codes = keep.tile([P, words], U32, name=name + "_codes", align_bytes=64)
-            plane = keep.tile([P, words], U8, name=name + "_plane", align_bytes=64)
+        def quantise(src, words, name, tag=""):
+            codes = keep.tile([P, words], U32, name=name + "_codes", tag=tag, align_bytes=ALIGN)
+            plane = keep.tile([P, words], U8, name=name + "_plane", align_bytes=ALIGN)
             nc.vector.quantize_mx(out=codes[:].bitcast(FP8X4), scales=plane[:], in_=src)
             return codes, plane
 
-        def quantise_w1(b, a, t):
-            codes, plane = quantise(w1_grouped[b, a, t][:], P, "w1_%d%d%d" % (b, a, t))
-            w1_codes[b, a, t], w1_plane[b, a, t] = codes[:], plane[:]
+        def round_w1(b, a, t, copy, dst):
+            copy(
+                dst.rearrange("p (q u i j) -> p q u j i", u=2, i=RUN // 2, j=PACK),
+                w1_raw[b, a][:].rearrange("p j (q t u i) -> p t q u j i", t=PACK, u=2, i=RUN // 2)[:, t],
+            )
+
+        def round_early_w1(a, t, copy):
+            w1_rounded[a, t] = keep.tile(
+                [P, PASS], BF16, name="w1_rounded", tag="w1_rounded%d%d" % (a, t), align_bytes=ALIGN
+            )
+            round_w1(0, a, t, copy, w1_rounded[a, t][:])
+
+        def quantise_early_w1(a, t):
+            codes, plane = quantise(w1_rounded[a, t][:], P, "w1_early%d%d" % (a, t))
+            w1_codes[a, t], w1_plane[a, t] = codes[:], plane[:]
 
         def late_w1(t):
-            both = keep.tile([P, K_PASSES * PASS], BF16, name="w1_both", tag="w1_both", bufs=2, align_bytes=64)
+            both = keep.tile([P, K_PASSES * PASS], BF16, name="w1_both", tag="w1_both", bufs=2, align_bytes=ALIGN)
             for a in range(K_PASSES):
                 round_w1(1, a, t, nc.scalar.copy, both[:, a * PASS : (a + 1) * PASS])
             codes, plane = quantise(both[:], K_PASSES * P, "w1_late%d" % t)
             for a in range(K_PASSES):
-                w1_codes[1, a, t], w1_plane[1, a, t] = codes[:, a * P : (a + 1) * P], plane[:, a * P : (a + 1) * P]
+                cols = slice(a * P, (a + 1) * P)
+                w1_codes[a, PACK + t], w1_plane[a, PACK + t] = codes[:, cols], plane[:, cols]
 
-        steps = [(a, t) for a in range(K_PASSES) for t in range(PACK)]
-        for n, (a, t) in enumerate(steps):
-            w1_grouped[0, a, t] = keep.tile([P, PASS], BF16, name="w1_grouped", tag="w1_grouped", bufs=4, align_bytes=64)
-            round_w1(0, a, t, nc.vector.tensor_copy, w1_grouped[0, a, t][:])
-            if n > 0:
-                quantise_w1(0, *steps[n - 1])
-        quantise_w1(0, *steps[-1])
+        steps = [(0, t) for t in range(PACK)] + [(1, t) for t in range(lead)]
+        for step, (a, t) in enumerate(steps):
+            round_early_w1(a, t, nc.vector.tensor_copy)
+            if step > 0:
+                quantise_early_w1(*steps[step - 1])
+        quantise_early_w1(*steps[-1])
 
-        late_tanh = shared.tile([P, PACK * S], F32, name="late_tanh", offset=0)
+        deal_w4(0, lead, PACK, "w1_rounded10")
+        deal_w4(1, 0, PACK, "w4_last")
+        load_w1(1, 0, "staged")
+        load_w1(1, 1, "w1_first")
+
+        late_tanh = shared.tile([P, PACK * S], F32, name="late_tanh", offset=LATE_TANH_AT, align_bytes=ALIGN)
         tanh_b, h = {}, {}
+
+        def first_stage_pass(acc, codes, plane, a, s, start, stop):
+            nc.tensor.matmul_mx(
+                out=acc[:],
+                lhsT=codes,
+                lhsT_scale=plane,
+                rhs=v_words[a, s][:].bitcast(FP8X4),
+                rhs_scale=planes[:, a, s * BANK : (s + 1) * BANK],
+                start=start,
+                stop=stop,
+            )
 
         def tanh_tile(n):
             if n < PACK:
-                tanh_b[n] = keep.tile([P, S], F32, name="tanh%d" % n, tag="tanh%d" % n, align_bytes=64)[:]
+                tanh_b[n] = keep.tile([P, S], F32, name="tanh%d" % n, tag="tanh%d" % n, align_bytes=ALIGN)[:]
             else:
                 tanh_b[n] = late_tanh[:, (n - PACK) * S : (n - PACK + 1) * S]
             for s in range(HALVES):
-                acc = psum.tile([P, BANK], F32, name="acc_b", tag="b")
+                acc = psum.tile([P, BANK], F32, name="acc_b", tag=bank_tag(1 if n == 1 else 0, s))
                 for a in range(K_PASSES):
-                    nc.tensor.matmul_mx(
-                        out=acc[:],
-                        lhsT=w4_codes[:, a * ROW_TILES + n, :].bitcast(FP4X4),
-                        lhsT_scale=w4_plane[:, a * ROW_TILES + n, :],
-                        rhs=v_words[a, s][:].bitcast(FP8X4),
-                        rhs_scale=v_scales[a][:, s * BANK : (s + 1) * BANK],
-                        start=(a == 0),
-                        stop=(a == K_PASSES - 1),
-                    )
+                    plane = planes[:, a, S + n * P : S + (n + 1) * P]
+                    first_stage_pass(acc, w4_codes[a, n].bitcast(FP4X4), plane, a, s, a == 0, a == K_PASSES - 1)
                 nc.scalar.activation(tanh_b[n][:, s * BANK : (s + 1) * BANK], acc[:], ACT.Tanh)
 
         def h_tile(n):
-            b, t = divmod(n, PACK)
+            order = (0, 1) if n == 0 else (1, 0)
             h[n] = keep.tile([P, S], F32, name="h%d" % n)
             for s in range(HALVES):
-                acc = psum.tile([P, BANK], F32, name="acc_a", tag="a")
-                for a in range(K_PASSES):
-                    nc.tensor.matmul_mx(
-                        out=acc[:],
-                        lhsT=w1_codes[b, a, t].bitcast(FP8X4),
-                        lhsT_scale=w1_plane[b, a, t],
-                        rhs=v_words[a, s][:].bitcast(FP8X4),
-                        rhs_scale=v_scales[a][:, s * BANK : (s + 1) * BANK],
-                        start=(a == 0),
-                        stop=(a == K_PASSES - 1),
-                    )
+                acc = psum.tile([P, BANK], F32, name="acc_a", tag=bank_tag((2, 3, 1)[n % 3], s))
+                for a in order:
+                    codes = w1_codes[a, n].bitcast(FP8X4)
+                    first_stage_pass(acc, codes, w1_plane[a, n], a, s, a == order[0], a == order[-1])
                 cols = slice(s * BANK, (s + 1) * BANK)
                 nc.vector.scalar_tensor_tensor(
-                    h[n][:, cols], acc[:], consts[:, b, t : t + 1], tanh_b[n][:, cols], ALU.max, ALU.mult
+                    h[n][:, cols], acc[:], consts[:, n, 0:1], tanh_b[n][:, cols], ALU.max, ALU.mult
                 )
 
-        south, south_planes, xs, x2 = {}, {}, {}, {}
+        south, south_rounded, signed, xs, x2 = {}, {}, {}, {}, {}
 
         def pick_south(n):
             b, t = divmod(n, PACK)
             if t == 0:
-                south[b] = keep.tile([P, PACK * M], F32, name="south%d" % b, tag="tab%d" % b, align_bytes=64)
-                south_planes[b] = keep.tile(
-                    [P, PACK * M], BF16, name="south_planes%d" % b, tag="tanh%d" % (3 * b), align_bytes=64
+                south[b] = keep.tile([P, PACK * M], F32, name="south%d" % b, tag="tab%d" % b, align_bytes=ALIGN)
+                south_rounded[b] = keep.tile(
+                    [P, PACK * M], BF16, name="south_rounded%d" % b, tag=("tanh0", "tanh3")[b], align_bytes=ALIGN
                 )
             cols = slice(t * M, (t + 1) * M)
             nc.vector.tensor_copy(south[b][:, cols], h[n][:].indirect(pos2_sb[:]))
-            nc.scalar.activation(
-                south_planes[b][:, cols], south[b][:, cols], ACT.Copy, scale=consts[:, b, PACK + t : PACK + t + 1]
-            )
+            nc.scalar.activation(south_rounded[b][:, cols], south[b][:, cols], ACT.Copy, scale=consts[:, n, 1:2])
 
         def weave(dst, src):
             nc.scalar.copy(
@@ -224,86 +264,110 @@ def tile_list_isogloss_shared_features_kernel(
                 src.rearrange("p (t c i) -> p c t i", i=4, t=PACK),
             )
 
-        def quantise_south(b):
-            tags = ("tanh1", "tanh2") if b == 0 else ("signed", "magnitude")
-            signed = keep.tile([P, PACK * M], BF16, name="signed%d" % b, tag=tags[0], align_bytes=64)
-            magnitude = keep.tile([P, PACK * M], BF16, name="magnitude%d" % b, tag=tags[1], align_bytes=64)
-            weave(signed[:], south_planes[b][:])
-            nc.scalar.activation(magnitude[:], signed[:], ACT.Abs)
-            xs[b] = quantise(signed[:], M, "xs%d" % b)
+        def south_tile(name, b, offset, tag):
+            if b == 0:
+                return shared.tile([P, PACK * M], BF16, name=name, offset=offset, align_bytes=ALIGN)
+            return keep.tile([P, PACK * M], BF16, name=name, tag=tag, align_bytes=ALIGN)
+
+        def weave_signed(b):
+            signed[b] = south_tile("signed%d" % b, b, SIGNED_AT, "tanh1")
+            weave(signed[b][:], south_rounded[b][:])
+
+        def quantise_magnitude(b):
+            magnitude = south_tile("magnitude%d" % b, b, MAGNITUDE_AT, "tanh2")
+            nc.scalar.activation(magnitude[:], signed[b][:], ACT.Abs)
             x2[b] = quantise(magnitude[:], M, "x2%d" % b)
 
-        tanh_tile(0)
-        tanh_tile(1)
+        for n in range(lead):
+            tanh_tile(n)
+        for t in range(lead, PACK):
+            round_early_w1(1, t, nc.scalar.copy)
         for n in range(ROW_TILES):
             h_tile(n)
-            if n + 2 < ROW_TILES:
-                tanh_tile(n + 2)
+            if n + lead < PACK:
+                quantise_early_w1(1, n + lead)
+            if n + lead < ROW_TILES:
+                tanh_tile(n + lead)
             if n < PACK:
                 late_w1(n)
             if n > 0:
                 pick_south(n - 1)
-            if n == PACK:
-                quantise_south(0)
+            if n + lead == ROW_TILES - 1:
+                weave_signed(0)
+                xs[0] = quantise(signed[0][:], M, "xs0")
+                quantise_magnitude(0)
         pick_south(ROW_TILES - 1)
-        quantise_south(1)
+        weave_signed(1)
 
-        groups = ((0, 3), (3, 4))
-        woven, x1 = {}, {}
+        north_woven, x1, sums = {}, {}, {}
 
         def pick_north(g, b):
-            m0, m1 = groups[g]
+            m0, m1 = NORTH_GROUPS[g]
             width = (m1 - m0) * P
-            north = shared.tile([P, PACK * width], F32, name="north%d%d" % (g, b), offset=b * 2 * S * 4)
+            north = shared.tile(
+                [P, PACK * width], F32, name="north%d%d" % (g, b), offset=NORTH_AT[b], align_bytes=ALIGN
+            )
+            entries = pos1_sb[:, m0 * P // LIST_ROWS : m1 * P // LIST_ROWS]
             for t in range(PACK):
-                nc.vector.tensor_copy(
-                    north[:, t * width : (t + 1) * width], h[b * PACK + t][:].indirect(pos1_sb[:, 8 * m0 : 8 * m1])
-                )
-            woven[g, b] = keep.tile([P, PACK * width], BF16, name="north_woven%d%d" % (g, b), align_bytes=64)
-            weave(woven[g, b][:], north[:])
+                nc.vector.tensor_copy(north[:, t * width : (t + 1) * width], h[b * PACK + t][:].indirect(entries))
+            north_woven[g, b] = keep.tile(
+                [P, PACK * width], BF16, name="north_woven", tag="north_woven%d%d" % (g, b), align_bytes=ALIGN
+            )
+            weave(north_woven[g, b][:], north[:])
 
         def quantise_north(g, b):
-            m0, m1 = groups[g]
-            codes, plane = quantise(woven[g, b][:], (m1 - m0) * P, "x1_%d%d" % (g, b))
+            m0, m1 = NORTH_GROUPS[g]
+            codes, plane = quantise(north_woven[g, b][:], (m1 - m0) * P, "x1_%d%d" % (g, b))
             for m in range(m0, m1):
                 cols = slice((m - m0) * P, (m - m0 + 1) * P)
                 x1[m, b] = codes[:, cols], plane[:, cols]
 
-        sums = {}
+        pieces = {m: [(0, M)] for m in range(M_TILES - 1)}
+        pieces[M_TILES - 1] = [(0, M // 2), (M // 2, M)]
 
         def multiply(g, b):
-            for m in range(*groups[g]):
-                for tag, south_q in (("b", xs), ("a", x2)):
-                    if b == 0:
-                        sums[m, tag] = psum.tile([P, M], F32, name="acc_" + tag, tag=tag)
-                    nc.tensor.matmul_mx(
-                        out=sums[m, tag][:],
-                        lhsT=x1[m, b][0].bitcast(FP8X4),
-                        lhsT_scale=x1[m, b][1],
-                        rhs=south_q[b][0][:].bitcast(FP8X4),
-                        rhs_scale=south_q[b][1][:],
-                        start=(b == 0),
-                        stop=(b == R_PASSES - 1),
-                    )
+            for m in range(*NORTH_GROUPS[g]):
+                halved = len(pieces[m]) > 1
+                for piece, (c0, c1) in enumerate(pieces[m]):
+                    if b == 0 and halved:
+                        d_and_e = psum.tile([P, 2, c1 - c0], F32, name="d_and_e", tag=bank_tag(m, piece))
+                        sums[m, piece] = [d_and_e[:, 0, :], d_and_e[:, 1, :]]
+                    elif b == 0:
+                        sums[m, piece] = [
+                            psum.tile([P, M], F32, name="d_or_e", tag=bank_tag(m, which))[:] for which in range(2)
+                        ]
+                    for which, south_q in enumerate((xs, x2)):
+                        nc.tensor.matmul_mx(
+                            out=sums[m, piece][which],
+                            lhsT=x1[m, b][0].bitcast(FP8X4),
+                            lhsT_scale=x1[m, b][1],
+                            rhs=south_q[b][0][:, c0:c1].bitcast(FP8X4),
+                            rhs_scale=south_q[b][1][:, c0:c1],
+                            start=(b == 0 and not (halved and which == 1)),
+                            stop=(b == R_PASSES - 1 and not (halved and which == 0)),
+                        )
 
         def score(m):
-            weight = keep.tile([P, M], F32, name="weight", tag="weight", bufs=2)
-            nc.scalar.activation(weight[:], sums[m, "b"][:], ACT.Sigmoid)
-            result = keep.tile([P, M], F32, name="result%d" % m)
-            nc.vector.tensor_tensor(result[:], sums[m, "a"][:], weight[:], ALU.mult)
-            nc.sync.dma_start(out=out[m * P : (m + 1) * P, :], in_=result[:])
+            for piece, (c0, c1) in enumerate(pieces[m]):
+                d, e = sums[m, piece]
+                weight = keep.tile([P, c1 - c0], F32, name="weight%d%d" % (m, piece))
+                nc.scalar.activation(weight[:], d, ACT.Sigmoid)
+                result = keep.tile([P, c1 - c0], F32, name="result%d%d" % (m, piece))
+                nc.vector.tensor_tensor(result[:], e, weight[:], ALU.mult)
+                nc.sync.dma_start(out=out[m * P : (m + 1) * P, c0:c1], in_=result[:])
 
         pick_north(0, 0)
-        pick_north(0, 1)
         quantise_north(0, 0)
         multiply(0, 0)
-        pick_north(1, 0)
+        xs[1] = quantise(signed[1][:], M, "xs1", tag="north_woven00")
+        quantise_magnitude(1)
+        pick_north(0, 1)
         quantise_north(0, 1)
         multiply(0, 1)
-        pick_north(1, 1)
-        quantise_north(1, 0)
-        multiply(1, 0)
-        quantise_north(1, 1)
-        multiply(1, 1)
+        for b in range(R_PASSES):
+            pick_north(1, b)
+        for b in range(R_PASSES):
+            quantise_north(1, b)
+            multiply(1, b)
         for m in range(M_TILES):
             score(m)

from contextlib import ExitStack

import concourse.mybir as mybir
from concourse.masks import make_identity

K, H, T, S, M = 1024, 1024, 4096, 1024, 512
FLOPS = 2 * (2 * K * H * S + 2 * H * M * M)

F32 = mybir.dt.float32
BF16 = mybir.dt.bfloat16
I32 = mybir.dt.int32
U32 = mybir.dt.uint32
U16 = mybir.dt.uint16
U8 = mybir.dt.uint8
FP8X4 = mybir.dt.float8_e4m3fn_x4
FP4X4 = mybir.dt.float4_e2m1fn_x4
ACT = mybir.ActivationFunctionType
ALU = mybir.AluOpType

P = 128
PACK = 4
PASS = P * PACK
RUN = 8
BANK = 512
LIST_ROWS = 16
QUADRANT = 32
SCALE_ROWS = PASS // 32
K_PASSES = K // PASS
R_PASSES = H // PASS
HALVES = S // BANK
ROW_TILES = R_PASSES * PACK
M_TILES = M // P
ALIGN = 64

LATE_TANH_AT = 0
SIGNED_AT = PACK * S * 4
MAGNITUDE_AT = SIGNED_AT + PACK * M * 2
NORTH_AT = (LATE_TANH_AT, SIGNED_AT - 1024)

NORTH_GROUPS = ((0, M_TILES - 1), (M_TILES - 1, M_TILES))


def tile_list_isogloss_shared_features_kernel(
    tc, tab_words, tab_scales, offs, pos1, pos2, w1, w4_words, w4_scales, low, gain, out
):
    nc = tc.nc
    with ExitStack() as ctx:
        keep = ctx.enter_context(tc.tile_pool(name="keep", bufs=1))
        shared = ctx.enter_context(tc.tile_pool(name="shared", bufs=1))
        psum = ctx.enter_context(tc.psum_pool(name="psum", bufs=1))

        def bank_tag(pair, which):
            return "bank%d" % (2 * pair + which)

        offs_sb = keep.tile([P, S // LIST_ROWS], U16, name="offs_sb")
        pos1_sb = keep.tile([P, M // LIST_ROWS], U16, name="pos1_sb")
        pos2_sb = keep.tile([P, M // LIST_ROWS], U16, name="pos2_sb")

        all_rows = K_PASSES * SCALE_ROWS
        tab_rows = keep.tile([P, T], U8, name="tab_rows", align_bytes=ALIGN)
        nc.vector.memset(tab_rows[all_rows : P // 2, :].bitcast(I32), 0)
        nc.vector.memset(tab_rows[P // 2 : P, :].bitcast(I32), 0)
        w4_rows = keep.tile([all_rows, H // 4], I32, name="w4_rows")
        planes = keep.tile([P, K_PASSES, S + H], U8, name="planes", align_bytes=ALIGN)
        nc.gpsimd.memset(planes[:].bitcast(I32), 0)
        vectors = keep.tile([2, H], F32, name="vectors")
        vectors_dealt = keep.tile([P, H], F32, name="vectors_dealt")
        nc.gpsimd.memset(vectors_dealt[:], 0.0)
        ident = keep.tile([P, P], F32, name="ident")
        make_identity(nc, ident[:])

        warm_in = keep.tile([P, 1], F32, name="warm_in")
        warm_out = keep.tile([P, 1], F32, name="warm_out")
        nc.vector.memset(warm_in[:], 0.0)
        nc.scalar.activation(warm_out[:], warm_in[:], ACT.Sigmoid)

        tab = [keep.tile([P, T], I32, name="tab%d" % a, tag="tab%d" % a, align_bytes=ALIGN) for a in range(K_PASSES)]
        w4_raw = [keep.tile([P, K_PASSES, 2 * PASS // 4], I32, name="w4_raw%d" % b) for b in range(R_PASSES)]
        w1_raw = {}

        def load_tab(a):
            nc.sync.dma_start(out=tab[a][:], in_=tab_words[a].rearrange("p t i -> p (t i)").bitcast(I32))

        def load_w1(b, a, tag):
            w1_raw[b, a] = keep.tile([P, PACK, PASS], F32, name="w1_raw%d%d" % (b, a), tag=tag)
            nc.sync.dma_start(
                out=w1_raw[b, a][:],
                in_=w1[a * PASS : (a + 1) * PASS, b * PASS : (b + 1) * PASS].rearrange("(p j) c -> p j c", j=PACK),
            )

        def load_w4(b):
            nc.sync.dma_start(
                out=w4_raw[b][:],
                in_=w4_words[:, :, b * 2 * PASS : (b + 1) * 2 * PASS].bitcast(I32).rearrange("a p c -> p a c"),
            )

        nc.sync.dma_start(offs_sb[:], offs)
        nc.sync.dma_start(
            out=tab_rows[0:all_rows, :].bitcast(I32), in_=tab_scales.bitcast(I32).rearrange("a q c -> (a q) c")
        )
        nc.sync.dma_start(out=w4_rows[:], in_=w4_scales.bitcast(I32).rearrange("a q c -> (a q) c"))
        for row, vec in enumerate((low, gain)):
            nc.sync.dma_start(out=vectors[row : row + 1, :], in_=vec.rearrange("(o r) -> o r", o=1))
        load_w4(0)
        load_tab(0)
        nc.sync.dma_start(pos2_sb[:], pos2)
        nc.sync.dma_start(pos1_sb[:], pos1)
        load_tab(1)
        load_w1(0, 0, "w1_first")
        load_w1(0, 1, "w1_second")
        load_w4(1)

        picked_rows = keep.tile([P, S], U8, name="picked_rows", align_bytes=ALIGN)
        nc.vector.tensor_copy(picked_rows[:], tab_rows[:].indirect(offs_sb[:]))
        staged = keep.tile([all_rows, (S + H) // 4], I32, name="staged", tag="staged")
        nc.vector.tensor_copy(
            staged[:, S // 4 :].rearrange("p (b t q w) -> p b t q w", b=R_PASSES, t=PACK, w=RUN // 4),
            w4_rows[:].rearrange("p (b q t w) -> p b t q w", b=R_PASSES, t=PACK, w=RUN // 4),
        )
        nc.vector.tensor_copy(staged[:, 0 : S // 4], picked_rows[0:all_rows, :].bitcast(I32))
        rows_per_quadrant = SCALE_ROWS // (P // QUADRANT)
        for a, queue in enumerate((nc.scalar, nc.gpsimd)):
            for r in range(rows_per_quadrant):
                queue.dma_start(
                    out=planes[r:P:QUADRANT, a, :].bitcast(I32),
                    in_=staged[SCALE_ROWS * a + r : SCALE_ROWS * (a + 1) : rows_per_quadrant, :],
                )

        v_words, w4_codes = {}, {}

        def gather_words(a):
            for s in range(HALVES):
                v_words[a, s] = keep.tile([P, BANK], U32, name="v_words%d%d" % (a, s), align_bytes=ALIGN)
                entries = offs_sb[:, s * BANK // LIST_ROWS : (s + 1) * BANK // LIST_ROWS]
                nc.vector.tensor_copy(v_words[a, s][:], tab[a][:].bitcast(U32).indirect(entries))

        def deal_w4(b, t0, t1, tag):
            dealt = keep.tile([P, K_PASSES * (t1 - t0), 2 * P], U8, name="w4_dealt", tag=tag, align_bytes=ALIGN)
            nc.vector.tensor_copy(
                dealt[:].bitcast(I32).rearrange("p (a t) (q w) -> p a t q w", a=K_PASSES, w=RUN // 2),
                w4_raw[b][:].rearrange("p a (q t w) -> p a t q w", t=PACK, w=RUN // 2)[:, :, t0:t1],
            )
            for a in range(K_PASSES):
                for t in range(t0, t1):
                    w4_codes[a, b * PACK + t] = dealt[:, a * (t1 - t0) + t - t0, :]

        lead = 2
        deal_w4(0, 0, lead, "w4_first")
        gather_words(0)
        gather_words(1)

        nc.scalar.copy(
            vectors_dealt[0:2, :].rearrange("p (b t q i) -> p b t q i", b=R_PASSES, t=PACK, i=RUN),
            vectors[:].rearrange("p (b q t i) -> p b t q i", b=R_PASSES, t=PACK, i=RUN),
        )
        consts = keep.tile([P, ROW_TILES, 2], F32, name="consts")
        for b in range(R_PASSES):
            turned = psum.tile([P, PACK, P], F32, name="turned", tag=bank_tag(3, b))
            for t in range(PACK):
                n = b * PACK + t
                nc.tensor.transpose(turned[:, t, :], vectors_dealt[:, n * P : (n + 1) * P], ident[:])
            nc.scalar.copy(consts[:, b * PACK : (b + 1) * PACK, :], turned[:, :, 0:2])

        w1_rounded, w1_codes, w1_plane = {}, {}, {}

        def quantise(src, words, name, tag=""):
            codes = keep.tile([P, words], U32, name=name + "_codes", tag=tag, align_bytes=ALIGN)
            plane = keep.tile([P, words], U8, name=name + "_plane", align_bytes=ALIGN)
            nc.vector.quantize_mx(out=codes[:].bitcast(FP8X4), scales=plane[:], in_=src)
            return codes, plane

        def round_w1(b, a, t, copy, dst):
            copy(
                dst.rearrange("p (q u i j) -> p q u j i", u=2, i=RUN // 2, j=PACK),
                w1_raw[b, a][:].rearrange("p j (q t u i) -> p t q u j i", t=PACK, u=2, i=RUN // 2)[:, t],
            )

        def round_early_w1(a, t, copy):
            w1_rounded[a, t] = keep.tile(
                [P, PASS], BF16, name="w1_rounded", tag="w1_rounded%d%d" % (a, t), align_bytes=ALIGN
            )
            round_w1(0, a, t, copy, w1_rounded[a, t][:])

        def quantise_early_w1(a, t):
            codes, plane = quantise(w1_rounded[a, t][:], P, "w1_early%d%d" % (a, t))
            w1_codes[a, t], w1_plane[a, t] = codes[:], plane[:]

        def late_w1(t):
            both = keep.tile([P, K_PASSES * PASS], BF16, name="w1_both", tag="w1_both", bufs=2, align_bytes=ALIGN)
            for a in range(K_PASSES):
                round_w1(1, a, t, nc.scalar.copy, both[:, a * PASS : (a + 1) * PASS])
            codes, plane = quantise(both[:], K_PASSES * P, "w1_late%d" % t)
            for a in range(K_PASSES):
                cols = slice(a * P, (a + 1) * P)
                w1_codes[a, PACK + t], w1_plane[a, PACK + t] = codes[:, cols], plane[:, cols]

        steps = [(0, t) for t in range(PACK)] + [(1, t) for t in range(lead)]
        for step, (a, t) in enumerate(steps):
            round_early_w1(a, t, nc.vector.tensor_copy)
            if step > 0:
                quantise_early_w1(*steps[step - 1])
        quantise_early_w1(*steps[-1])

        deal_w4(0, lead, PACK, "w1_rounded10")
        deal_w4(1, 0, PACK, "w4_last")
        load_w1(1, 0, "staged")
        load_w1(1, 1, "w1_first")

        late_tanh = shared.tile([P, PACK * S], F32, name="late_tanh", offset=LATE_TANH_AT, align_bytes=ALIGN)
        tanh_b, h = {}, {}

        def first_stage_pass(acc, codes, plane, a, s, start, stop):
            nc.tensor.matmul_mx(
                out=acc[:],
                lhsT=codes,
                lhsT_scale=plane,
                rhs=v_words[a, s][:].bitcast(FP8X4),
                rhs_scale=planes[:, a, s * BANK : (s + 1) * BANK],
                start=start,
                stop=stop,
            )

        def tanh_tile(n):
            if n < PACK:
                tanh_b[n] = keep.tile([P, S], F32, name="tanh%d" % n, tag="tanh%d" % n, align_bytes=ALIGN)[:]
            else:
                tanh_b[n] = late_tanh[:, (n - PACK) * S : (n - PACK + 1) * S]
            for s in range(HALVES):
                acc = psum.tile([P, BANK], F32, name="acc_b", tag=bank_tag(1 if n == 1 else 0, s))
                for a in range(K_PASSES):
                    plane = planes[:, a, S + n * P : S + (n + 1) * P]
                    first_stage_pass(acc, w4_codes[a, n].bitcast(FP4X4), plane, a, s, a == 0, a == K_PASSES - 1)
                nc.scalar.activation(tanh_b[n][:, s * BANK : (s + 1) * BANK], acc[:], ACT.Tanh)

        def h_tile(n):
            order = (0, 1) if n == 0 else (1, 0)
            h[n] = keep.tile([P, S], F32, name="h%d" % n)
            for s in range(HALVES):
                acc = psum.tile([P, BANK], F32, name="acc_a", tag=bank_tag((2, 3, 1)[n % 3], s))
                for a in order:
                    codes = w1_codes[a, n].bitcast(FP8X4)
                    first_stage_pass(acc, codes, w1_plane[a, n], a, s, a == order[0], a == order[-1])
                cols = slice(s * BANK, (s + 1) * BANK)
                nc.vector.scalar_tensor_tensor(
                    h[n][:, cols], acc[:], consts[:, n, 0:1], tanh_b[n][:, cols], ALU.max, ALU.mult
                )

        south, south_rounded, signed, xs, x2 = {}, {}, {}, {}, {}

        def pick_south(n):
            b, t = divmod(n, PACK)
            if t == 0:
                south[b] = keep.tile([P, PACK * M], F32, name="south%d" % b, tag="tab%d" % b, align_bytes=ALIGN)
                south_rounded[b] = keep.tile(
                    [P, PACK * M], BF16, name="south_rounded%d" % b, tag=("tanh0", "tanh3")[b], align_bytes=ALIGN
                )
            cols = slice(t * M, (t + 1) * M)
            nc.vector.tensor_copy(south[b][:, cols], h[n][:].indirect(pos2_sb[:]))
            nc.scalar.activation(south_rounded[b][:, cols], south[b][:, cols], ACT.Copy, scale=consts[:, n, 1:2])

        def weave(dst, src):
            nc.scalar.copy(
                dst.rearrange("p (c i t) -> p c t i", i=4, t=PACK),
                src.rearrange("p (t c i) -> p c t i", i=4, t=PACK),
            )

        def south_tile(name, b, offset, tag):
            if b == 0:
                return shared.tile([P, PACK * M], BF16, name=name, offset=offset, align_bytes=ALIGN)
            return keep.tile([P, PACK * M], BF16, name=name, tag=tag, align_bytes=ALIGN)

        def weave_signed(b):
            signed[b] = south_tile("signed%d" % b, b, SIGNED_AT, "tanh1")
            weave(signed[b][:], south_rounded[b][:])

        def quantise_magnitude(b):
            magnitude = south_tile("magnitude%d" % b, b, MAGNITUDE_AT, "tanh2")
            nc.scalar.activation(magnitude[:], signed[b][:], ACT.Abs)
            x2[b] = quantise(magnitude[:], M, "x2%d" % b)

        for n in range(lead):
            tanh_tile(n)
        for t in range(lead, PACK):
            round_early_w1(1, t, nc.scalar.copy)
        for n in range(ROW_TILES):
            h_tile(n)
            if n + lead < PACK:
                quantise_early_w1(1, n + lead)
            if n + lead < ROW_TILES:
                tanh_tile(n + lead)
            if n < PACK:
                late_w1(n)
            if n > 0:
                pick_south(n - 1)
            if n + lead == ROW_TILES - 1:
                weave_signed(0)
                xs[0] = quantise(signed[0][:], M, "xs0")
                quantise_magnitude(0)
        pick_south(ROW_TILES - 1)
        weave_signed(1)

        north_woven, x1, sums = {}, {}, {}

        def pick_north(g, b):
            m0, m1 = NORTH_GROUPS[g]
            width = (m1 - m0) * P
            north = shared.tile(
                [P, PACK * width], F32, name="north%d%d" % (g, b), offset=NORTH_AT[b], align_bytes=ALIGN
            )
            entries = pos1_sb[:, m0 * P // LIST_ROWS : m1 * P // LIST_ROWS]
            for t in range(PACK):
                nc.vector.tensor_copy(north[:, t * width : (t + 1) * width], h[b * PACK + t][:].indirect(entries))
            north_woven[g, b] = keep.tile(
                [P, PACK * width], BF16, name="north_woven", tag="north_woven%d%d" % (g, b), align_bytes=ALIGN
            )
            weave(north_woven[g, b][:], north[:])

        def quantise_north(g, b):
            m0, m1 = NORTH_GROUPS[g]
            codes, plane = quantise(north_woven[g, b][:], (m1 - m0) * P, "x1_%d%d" % (g, b))
            for m in range(m0, m1):
                cols = slice((m - m0) * P, (m - m0 + 1) * P)
                x1[m, b] = codes[:, cols], plane[:, cols]

        pieces = {m: [(0, M)] for m in range(M_TILES - 1)}
        pieces[M_TILES - 1] = [(0, M // 2), (M // 2, M)]

        def multiply(g, b):
            for m in range(*NORTH_GROUPS[g]):
                halved = len(pieces[m]) > 1
                for piece, (c0, c1) in enumerate(pieces[m]):
                    if b == 0 and halved:
                        d_and_e = psum.tile([P, 2, c1 - c0], F32, name="d_and_e", tag=bank_tag(m, piece))
                        sums[m, piece] = [d_and_e[:, 0, :], d_and_e[:, 1, :]]
                    elif b == 0:
                        sums[m, piece] = [
                            psum.tile([P, M], F32, name="d_or_e", tag=bank_tag(m, which))[:] for which in range(2)
                        ]
                    for which, south_q in enumerate((xs, x2)):
                        nc.tensor.matmul_mx(
                            out=sums[m, piece][which],
                            lhsT=x1[m, b][0].bitcast(FP8X4),
                            lhsT_scale=x1[m, b][1],
                            rhs=south_q[b][0][:, c0:c1].bitcast(FP8X4),
                            rhs_scale=south_q[b][1][:, c0:c1],
                            start=(b == 0 and not (halved and which == 1)),
                            stop=(b == R_PASSES - 1 and not (halved and which == 0)),
                        )

        def score(m):
            for piece, (c0, c1) in enumerate(pieces[m]):
                d, e = sums[m, piece]
                weight = keep.tile([P, c1 - c0], F32, name="weight%d%d" % (m, piece))
                nc.scalar.activation(weight[:], d, ACT.Sigmoid)
                result = keep.tile([P, c1 - c0], F32, name="result%d%d" % (m, piece))
                nc.vector.tensor_tensor(result[:], e, weight[:], ALU.mult)
                nc.sync.dma_start(out=out[m * P : (m + 1) * P, c0:c1], in_=result[:])

        pick_north(0, 0)
        quantise_north(0, 0)
        multiply(0, 0)
        xs[1] = quantise(signed[1][:], M, "xs1", tag="north_woven00")
        quantise_magnitude(1)
        pick_north(0, 1)
        quantise_north(0, 1)
        multiply(0, 1)
        for b in range(R_PASSES):
            pick_north(1, b)
        for b in range(R_PASSES):
            quantise_north(1, b)
            multiply(1, b)
        for m in range(M_TILES):
            score(m)
